import numpy as np
import ml_dtypes


def mxq(x, axis, fmt="e4m3"):
    dtype, down = {"e4m3": (ml_dtypes.float8_e4m3fn, 7), "e5m2": (ml_dtypes.float8_e5m2, 14)}[fmt]
    v = np.moveaxis(np.asarray(x, np.float32).astype(ml_dtypes.bfloat16).astype(np.float64), axis, -1)
    blocks = v.reshape(v.shape[:-1] + (-1, 32))
    amax = np.abs(blocks).max(-1, keepdims=True)
    byte = np.maximum(np.where(amax > 0, np.frexp(amax)[1] - 1 + 127, 0) - down, 1)
    scale = np.exp2(byte - 127.0)
    codes = (blocks / scale).astype(np.float32).astype(dtype).astype(np.float64)
    return np.moveaxis((codes * scale).reshape(v.shape), -1, axis)


WIDE = False


def mx_kscale(k):
    if not WIDE:
        return np.ones(k)
    levels = np.array([10, -10, 5, -5, 0])
    if k % 512:
        return np.exp2(np.random.permutation(np.resize(levels, k // 32))).repeat(32)
    a = np.empty((k // 512, 16))
    for p in range(k // 512):
        a[p, :8] = np.random.permutation(np.resize(levels, 8))
        for g in range(8):
            far = levels[np.abs(levels - a[p, g]) >= 10]
            a[p, g + 8] = far[np.random.randint(len(far))]
    return np.exp2(a.ravel()).repeat(32)


def f64(x):
    return np.asarray(x).astype(np.float64)


def striped(idx):
    return np.tile(idx.reshape(-1, 16).T, (8, 1)).astype(np.uint16)


def unstriped(offs):
    return offs[:16].T.reshape(-1).astype(np.int64)


def pack_weight(w):
    k, n = w.shape
    w = f64(np.asarray(w, np.float32).astype(ml_dtypes.bfloat16)).reshape(k // 32, 32, n)
    amax = np.abs(w).max(1)
    byte = np.clip(np.where(amax > 0, np.frexp(amax)[1] - 1 + 127 - 7, 1), 1, 254)
    scaled = (w * np.exp2(127.0 - byte)[:, None, :]).reshape(k, n).astype(np.float32)
    words = np.ascontiguousarray(scaled.reshape(k // 512, 128, 4, n).transpose(0, 1, 3, 2)).astype(ml_dtypes.float8_e4m3fn).view(np.uint8)
    return words, np.ascontiguousarray(byte.astype(np.uint8).reshape(k // 512, 16, n))


def unpack_weight(words, scales):
    g, p, n, _ = words.shape
    vals = np.ascontiguousarray(words).view(ml_dtypes.float8_e4m3fn).astype(np.float64) * np.repeat(np.exp2(scales.astype(np.float64) - 127.0), 8, axis=1)[..., None]
    return vals.transpose(0, 1, 3, 2).reshape(g * 512, n)


def relu(v):
    return np.maximum(v, 0.0)


K, T, S, N, D, V = 1024, 1024, 512, 128, 4, 256
P = 2 ** 7


def setup_inputs():
    n = np.random.standard_normal
    s = mx_kscale(K)[:, None]
    packed_xT = pack_weight(n((K, T)) * s)
    return {
        "x_words": packed_xT[0],
        "x_scales": packed_xT[1],
        "w1": (n((K, N)) / np.sqrt(K) / s).astype(np.float32),
        "w2": (n((K, N)) / np.sqrt(K) / s).astype(np.float32),
        "w3": (n((K, N)) / np.sqrt(K) / s).astype(np.float32),
        "tri": (np.tile(np.random.uniform(0.1, 0.6, (D, 1, V)), (1, P, 1))).astype(np.float32),
        "dist": (np.tile(np.random.uniform(0.2, 1.5, (D, 1, V)), (1, P, 1))).astype(np.float32),
        "offs": striped(np.random.permutation(T)[:S]),
        "pos1": striped(np.random.permutation(S)[:V]),
        "pos2": striped(np.random.permutation(S)[:V]),
        "pos3": striped(np.random.permutation(S)[:V]),
        "pos4": striped(np.random.permutation(S)[:V]),
    }


def reference(x_words, x_scales, w1, w2, w3, tri, dist, offs, pos1, pos2, pos3, pos4):
    xq = unpack_weight(x_words, x_scales)[:, unstriped(offs)]
    mean = mxq(f64(w2), 0, "e4m3").T @ xq
    mu = np.log(np.exp(mean) + 1.0)
    msq = mxq(f64(w3), 0, "e4m3").T @ xq
    var = np.abs((mu) ** 2 - (np.log(np.exp(msq) + 1.0))) + 0.05
    ch0 = f64(tri)[0, :1] * (var[:, unstriped(pos1)] / (var[:, unstriped(pos1)] + (relu(f64(dist)[0, :1] - mu[:, unstriped(pos1)])) ** 2))
    irr = mxq(f64(w1), 0, "e4m3").T @ xq
    er = np.exp(0.5 * irr)
    ch1 = f64(tri)[1, :1] * (var[:, unstriped(pos2)] / (var[:, unstriped(pos2)] + (relu(f64(dist)[1, :1] - mu[:, unstriped(pos2)])) ** 2))
    ch2 = f64(tri)[2, :1] * (var[:, unstriped(pos3)] / (var[:, unstriped(pos3)] + (relu(f64(dist)[2, :1] - mu[:, unstriped(pos3)])) ** 2))
    ch3 = f64(tri)[3, :1] * (var[:, unstriped(pos4)] / (var[:, unstriped(pos4)] + (relu(f64(dist)[3, :1] - mu[:, unstriped(pos4)])) ** 2))
    return np.log((ch0 * er[:, unstriped(pos1)] + ch1 * er[:, unstriped(pos2)] + ch2 * er[:, unstriped(pos3)] + ch3 * er[:, unstriped(pos4)]) / (ch0 + ch1 + ch2 + ch3 + 0.02) + 0.1)

@@ -1,0 +1,195 @@
+from contextlib import ExitStack
+
+import concourse.mybir as mybir
+from concourse.masks import make_identity
+
+K, T, S, M, D, V = 1024, 1024, 512, 128, 4, 256
+FLOPS = 3 * 2 * K * S * M
+P = 128
+PACK = 4
+PASSES = K // (P * PACK)
+HALVES = V // P
+TINY = 1e-15
+
+F32 = mybir.dt.float32
+BF16 = mybir.dt.bfloat16
+I32 = mybir.dt.int32
+U32 = mybir.dt.uint32
+U16 = mybir.dt.uint16
+U8 = mybir.dt.uint8
+FP8X4 = mybir.dt.float8_e4m3fn_x4
+ALU = mybir.AluOpType
+ACT = mybir.ActivationFunctionType
+
+
+def tile_picked_yddgi_log_p_kernel(
+    tc, x_words, x_scales, w1, w2, w3, tri, dist, offs, pos1, pos2, pos3, pos4, out
+):
+    nc = tc.nc
+    with ExitStack() as ctx:
+        lists = ctx.enter_context(tc.tile_pool(name="lists", bufs=1))
+        sb = ctx.enter_context(tc.tile_pool(name="sb", bufs=1))
+        psum = ctx.enter_context(tc.psum_pool(name="psum", bufs=1))
+
+        offs_sb = lists.tile([P, S // 16], U16, name="offs_sb")
+        nc.sync.dma_start(offs_sb[:], offs)
+        scales = sb.tile([P, T], U8, name="scales")
+        nc.gpsimd.memset(scales[:].bitcast(I32), 0)
+        words = [sb.tile([P, T], U32, name="words%d" % g) for g in range(PASSES)]
+
+        def load_words(g):
+            nc.sync.dma_start(words[g][:].bitcast(I32), x_words[g].rearrange("p n t -> p (n t)").bitcast(I32))
+
+        for q in range(4):
+            nc.sync.dma_start(
+                scales[32 * q : 32 * q + 4 * PASSES, :].bitcast(I32),
+                x_scales[:, 4 * q : 4 * q + 4, :].bitcast(I32),
+            )
+        load_words(0)
+        load_words(1)
+        raw = {}
+        for i, w in enumerate((w1, w2, w3)):
+            for g in range(PASSES):
+                tile = sb.tile([P, PACK, M], F32, name="raw%d_%d" % (i, g))
+                nc.sync.dma_start(tile[:], w[g * 512 : (g + 1) * 512, :].rearrange("(p j) m -> p j m", j=PACK))
+                raw[i, g] = tile[:]
+        pos_sb = []
+        for d, pos in enumerate((pos1, pos2, pos3, pos4)):
+            tile = lists.tile([P, V // 16], U16, name="pos_sb%d" % d)
+            nc.sync.dma_start(tile[:], pos)
+            pos_sb.append(tile)
+        dist_sb = sb.tile([P, D, V], F32, name="dist_sb")
+        nc.sync.dma_start(dist_sb[:], dist.rearrange("d p v -> p d v"))
+        tri_rows = sb.tile([P, P], F32, name="tri_rows")
+        nc.gpsimd.memset(tri_rows[:], 0.0)
+        nc.sync.dma_start(tri_rows[: D * HALVES, :], tri[:, 0, :].rearrange("d (h c) -> d h c", c=P))
+
+        ident = sb.tile([P, P], F32, name="ident")
+        make_identity(nc, ident[:])
+        neg_half = sb.tile([P, V], F32, name="neg_half")
+        nc.gpsimd.memset(neg_half[:], -0.5)
+        zero_exp = sb.tile([P, 1], F32, name="zero_exp", tag="mu")
+        nc.gpsimd.memset(zero_exp[:], 0.0)
+        one = sb.tile([P, 1], F32, name="one")
+        nc.scalar.activation(one[:], zero_exp[:], ACT.Exp, bias=zero_exp[:])
+        zero_ln = sb.tile([P, 1], F32, name="zero_ln", tag="vis0")
+        nc.gpsimd.memset(zero_ln[:], 0.0)
+
+        xs = sb.tile([P, S], U8, name="xs", align_bytes=64)
+        nc.vector.tensor_copy(xs[:], scales[:].indirect(offs_sb[:]))
+        xw = []
+        for g in range(PASSES):
+            tile = sb.tile([P, S], U32, name="xw%d" % g, align_bytes=64)
+            nc.vector.tensor_copy(tile[:], words[g][:].indirect(offs_sb[:]))
+            xw.append(tile)
+
+        acc = []
+        for i in range(3):
+            bank = psum.tile([P, S], F32, name="acc%d" % i, tag="bank%d" % i)
+            for g in range(PASSES):
+                grouped = sb.tile([P, M * PACK], BF16, name="grouped%d_%d" % (i, g), align_bytes=64)
+                dst = grouped[:].rearrange("p (c i t) -> p c t i", i=4, t=PACK)
+                src = raw[i, g].rearrange("p t (c i) -> p c t i", i=4)
+                if g == 0:
+                    nc.scalar.copy(dst, src)
+                else:
+                    nc.vector.tensor_copy(dst, src)
+                codes = sb.tile([P, M], U32, name="codes%d_%d" % (i, g), align_bytes=64)
+                wsc = sb.tile([P, M], U8, name="wsc%d_%d" % (i, g), align_bytes=64)
+                nc.vector.quantize_mx(out=codes[:].bitcast(FP8X4), scales=wsc[:], in_=grouped[:])
+                nc.tensor.matmul_mx(
+                    out=bank[:],
+                    lhsT=codes[:].bitcast(FP8X4),
+                    lhsT_scale=wsc[:],
+                    rhs=xw[g][:].bitcast(FP8X4),
+                    rhs_scale=xs[4 * g :, :],
+                    start=(g == 0),
+                    stop=(g == PASSES - 1),
+                )
+            acc.append(bank)
+
+        er = sb.tile([P, S], F32, name="er")
+        nc.scalar.activation(er[:], acc[0][:], ACT.Exp, bias=zero_exp[:], scale=0.5)
+        e_mean = sb.tile([P, S], F32, name="e_mean")
+        nc.scalar.activation(e_mean[:], acc[1][:], ACT.Exp, bias=zero_exp[:])
+        e_msq = sb.tile([P, S], F32, name="e_msq")
+        nc.scalar.activation(e_msq[:], acc[2][:], ACT.Exp, bias=zero_exp[:])
+
+        tri_ps = psum.tile([P, P], F32, name="tri_ps", tag="bank0")
+        nc.tensor.transpose(tri_ps[:], tri_rows[:], ident[:])
+        tri_col = sb.tile([P, D * HALVES], F32, name="tri_col")
+        nc.vector.tensor_copy(tri_col[:], tri_ps[:, : D * HALVES])
+
+        er_g = sb.tile([P, D, V], F32, name="er_g")
+        er_t = [psum.tile([P, 2 * HALVES, P], F32, name="er_t%d" % b, tag="bank%d" % (3 + b)) for b in range(2)]
+        for d in range(D):
+            nc.vector.tensor_copy(er_g[:, d, :], er[:].indirect(pos_sb[d][:]))
+            for h in range(HALVES):
+                nc.tensor.transpose(er_t[d // 2][:, (d % 2) * HALVES + h, :], er_g[:, d, h * P : (h + 1) * P], ident[:])
+
+        mu = sb.tile([P, S], F32, name="mu", tag="mu")
+        nc.scalar.activation(mu[:], e_mean[:], ACT.Ln, bias=one[:])
+        sp = sb.tile([P, S], F32, name="sp")
+        nc.scalar.activation(sp[:], e_msq[:], ACT.Ln, bias=one[:])
+        musq = sb.tile([P, S], F32, name="musq", tag="late_gap")
+        nc.scalar.activation(musq[:], mu[:], ACT.Square)
+
+        log_a = sb.tile([P, D, V], F32, name="log_a")
+
+        def log_shadow(d, gap):
+            nc.vector.tensor_tensor(gap, mu[:].indirect(pos_sb[d][:]), dist_sb[:, d, :], ALU.subtract)
+            a = sb.tile([P, V], F32, name="a%d" % d)
+            nc.vector.tensor_scalar(a[:], gap, -1.0, TINY, ALU.mult, ALU.max)
+            nc.scalar.activation(log_a[:, d, :], a[:], ACT.Ln, bias=zero_ln[:])
+
+        early_gap = sb.tile([P, 2, V], F32, name="early_gap")
+        for d in range(2):
+            log_shadow(d, early_gap[:, d, :])
+        diff = sb.tile([P, S], F32, name="diff")
+        nc.vector.tensor_tensor(diff[:], musq[:], sp[:], ALU.subtract)
+        adiff = sb.tile([P, S], F32, name="adiff")
+        nc.scalar.activation(adiff[:], diff[:], ACT.Abs)
+        log_var = sb.tile([P, S], F32, name="log_var")
+        nc.scalar.activation(log_var[:], adiff[:], ACT.Ln, bias=0.05)
+        late_gap = sb.tile([P, 2, V], F32, name="late_gap", tag="late_gap")
+        for d in range(2, D):
+            log_shadow(d, late_gap[:, d - 2, :])
+
+        y = sb.tile([P, D, V], F32, name="y")
+        num = psum.tile([P, V], F32, name="num", tag="bank0")
+        den = psum.tile([P, V], F32, name="den", tag="bank1")
+        z_t = [psum.tile([P, 2 * HALVES, P], F32, name="z_t%d" % b, tag="bank%d" % (5 + b)) for b in range(2)]
+        for b in range(2):
+            for s in range(2 * HALVES):
+                d, h = 2 * b + s // HALVES, s % HALVES
+                nc.tensor.matmul(z_t[b][:, s, :], log_a[:, d, h * P : (h + 1) * P], ident[:],
+                                 start=(s == 0), stop=False, is_transpose=True)
+        for d in range(D):
+            nc.vector.tensor_tensor(y[:, d, :], log_var[:].indirect(pos_sb[d][:]), neg_half[:], ALU.mult)
+            for h in range(HALVES):
+                s = (d % 2) * HALVES + h
+                nc.tensor.matmul(z_t[d // 2][:, s, :], y[:, d, h * P : (h + 1) * P], ident[:],
+                                 start=False, stop=(s == 2 * HALVES - 1), is_transpose=True)
+        for b in range(2):
+            vis = sb.tile([P, 2 * HALVES, P], F32, name="vis%d" % b, tag="vis%d" % b)
+            nc.scalar.activation(vis[:], z_t[b][:], ACT.Sigmoid, scale=-2.0)
+            ch = sb.tile([P, 2 * HALVES, P], F32, name="ch%d" % b)
+            for s in range(2 * HALVES):
+                c = 2 * HALVES * b + s
+                nc.vector.tensor_scalar(ch[:, s, :], vis[:, s, :], tri_col[:, c : c + 1], None, ALU.mult)
+            lit = sb.tile([P, 2 * HALVES, P], F32, name="lit%d" % b)
+            nc.vector.scalar_tensor_tensor(lit[:], er_t[b][:], 0.1, ch[:], ALU.add, ALU.mult)
+            for bank, terms in ((den, ch), (num, lit)):
+                for s in range(2 * HALVES):
+                    h = s % HALVES
+                    nc.tensor.matmul(bank[:, h * P : (h + 1) * P], terms[:, s, :], ident[:],
+                                     start=(b == 0 and s == 0), stop=(b == 1 and s == 2 * HALVES - 1),
+                                     is_transpose=True)
+
+        log_den = sb.tile([P, V], F32, name="log_den")
+        nc.scalar.activation(log_den[:], den[:], ACT.Ln, bias=0.02)
+        log_num = sb.tile([P, V], F32, name="log_num")
+        nc.scalar.activation(log_num[:], num[:], ACT.Ln, bias=0.002)
+        res = sb.tile([P, V], F32, name="res")
+        nc.vector.tensor_tensor(res[:], log_num[:], log_den[:], ALU.subtract)
+        nc.sync.dma_start(out, res[:])

@@ -9,7 +9,7 @@ P = 128
 PACK = 4
 PASSES = K // (P * PACK)
 HALVES = V // P
-TINY = 1e-15
+TINY = 2.0**-50
 
 F32 = mybir.dt.float32
 BF16 = mybir.dt.bfloat16
@@ -48,11 +48,15 @@ def tile_picked_yddgi_log_p_kernel(
         load_words(0)
         load_words(1)
         raw = {}
-        for i, w in enumerate((w1, w2, w3)):
+        for i, w in enumerate((w1, w2)):
+            tile = sb.tile([P, PASSES, PACK, M], F32, name="raw%d" % i)
+            nc.sync.dma_start(tile[:], w.rearrange("(g p j) m -> p g j m", p=P, j=PACK))
             for g in range(PASSES):
-                tile = sb.tile([P, PACK, M], F32, name="raw%d_%d" % (i, g))
-                nc.sync.dma_start(tile[:], w[g * 512 : (g + 1) * 512, :].rearrange("(p j) m -> p j m", j=PACK))
-                raw[i, g] = tile[:]
+                raw[i, g] = tile[:, g]
+        for g in range(PASSES):
+            tile = sb.tile([P, PACK, M], F32, name="raw2_%d" % g)
+            nc.sync.dma_start(tile[:], w3[g * 512 : (g + 1) * 512, :].rearrange("(p j) m -> p j m", j=PACK))
+            raw[2, g] = tile[:]
         pos_sb = []
         for d, pos in enumerate((pos1, pos2, pos3, pos4)):
             tile = lists.tile([P, V // 16], U16, name="pos_sb%d" % d)
@@ -72,8 +76,8 @@ def tile_picked_yddgi_log_p_kernel(
         nc.gpsimd.memset(zero_exp[:], 0.0)
         one = sb.tile([P, 1], F32, name="one")
         nc.scalar.activation(one[:], zero_exp[:], ACT.Exp, bias=zero_exp[:])
-        zero_ln = sb.tile([P, 1], F32, name="zero_ln", tag="vis0")
-        nc.gpsimd.memset(zero_ln[:], 0.0)
+        tiny = sb.tile([P, 1], F32, name="tiny", tag="vis0")
+        nc.gpsimd.memset(tiny[:], TINY)
 
         xs = sb.tile([P, S], U8, name="xs", align_bytes=64)
         nc.vector.tensor_copy(xs[:], scales[:].indirect(offs_sb[:]))
@@ -87,7 +91,7 @@ def tile_picked_yddgi_log_p_kernel(
         for i in range(3):
             bank = psum.tile([P, S], F32, name="acc%d" % i, tag="bank%d" % i)
             for g in range(PASSES):
-                grouped = sb.tile([P, M * PACK], BF16, name="grouped%d_%d" % (i, g), align_bytes=64)
+                grouped = sb.tile([P, M * PACK], BF16, name="grouped%d_%d" % (i, g), tag="grouped%d" % ((2 * i + g) % 3), align_bytes=64)
                 dst = grouped[:].rearrange("p (c i t) -> p c t i", i=4, t=PACK)
                 src = raw[i, g].rearrange("p t (c i) -> p c t i", i=4)
                 if g == 0:
@@ -115,7 +119,7 @@ def tile_picked_yddgi_log_p_kernel(
         e_msq = sb.tile([P, S], F32, name="e_msq")
         nc.scalar.activation(e_msq[:], acc[2][:], ACT.Exp, bias=zero_exp[:])
 
-        tri_ps = psum.tile([P, P], F32, name="tri_ps", tag="bank0")
+        tri_ps = psum.tile([P, P], F32, name="tri_ps", tag="bank2")
         nc.tensor.transpose(tri_ps[:], tri_rows[:], ident[:])
         tri_col = sb.tile([P, D * HALVES], F32, name="tri_col")
         nc.vector.tensor_copy(tri_col[:], tri_ps[:, : D * HALVES])
@@ -139,8 +143,8 @@ def tile_picked_yddgi_log_p_kernel(
         def log_shadow(d, gap):
             nc.vector.tensor_tensor(gap, mu[:].indirect(pos_sb[d][:]), dist_sb[:, d, :], ALU.subtract)
             a = sb.tile([P, V], F32, name="a%d" % d)
-            nc.vector.tensor_scalar(a[:], gap, -1.0, TINY, ALU.mult, ALU.max)
-            nc.scalar.activation(log_a[:, d, :], a[:], ACT.Ln, bias=zero_ln[:])
+            nc.vector.tensor_scalar(a[:], gap, -1.0, 0.0, ALU.mult, ALU.max)
+            nc.scalar.activation(log_a[:, d, :], a[:], ACT.Ln, bias=tiny[:])
 
         early_gap = sb.tile([P, 2, V], F32, name="early_gap")
         for d in range(2):
@@ -156,40 +160,40 @@ def tile_picked_yddgi_log_p_kernel(
             log_shadow(d, late_gap[:, d - 2, :])
 
         y = sb.tile([P, D, V], F32, name="y")
-        num = psum.tile([P, V], F32, name="num", tag="bank0")
-        den = psum.tile([P, V], F32, name="den", tag="bank1")
-        z_t = [psum.tile([P, 2 * HALVES, P], F32, name="z_t%d" % b, tag="bank%d" % (5 + b)) for b in range(2)]
-        for b in range(2):
-            for s in range(2 * HALVES):
-                d, h = 2 * b + s // HALVES, s % HALVES
-                nc.tensor.matmul(z_t[b][:, s, :], log_a[:, d, h * P : (h + 1) * P], ident[:],
-                                 start=(s == 0), stop=False, is_transpose=True)
+        num = psum.tile([P, V], F32, name="num", tag="bank5")
+        den = psum.tile([P, V], F32, name="den", tag="bank6")
+        z_t = [psum.tile([P, HALVES, P], F32, name="z_t%d" % d, tag="bank%d" % (0, 1, 2, 7)[d]) for d in range(D)]
+        for d in range(D):
+            for h in range(HALVES):
+                nc.tensor.matmul(z_t[d][:, h, :], log_a[:, d, h * P : (h + 1) * P], ident[:],
+                                 start=(h == 0), stop=False, is_transpose=True)
         for d in range(D):
             nc.vector.tensor_tensor(y[:, d, :], log_var[:].indirect(pos_sb[d][:]), neg_half[:], ALU.mult)
             for h in range(HALVES):
-                s = (d % 2) * HALVES + h
-                nc.tensor.matmul(z_t[d // 2][:, s, :], y[:, d, h * P : (h + 1) * P], ident[:],
-                                 start=False, stop=(s == 2 * HALVES - 1), is_transpose=True)
-        for b in range(2):
-            vis = sb.tile([P, 2 * HALVES, P], F32, name="vis%d" % b, tag="vis%d" % b)
-            nc.scalar.activation(vis[:], z_t[b][:], ACT.Sigmoid, scale=-2.0)
-            ch = sb.tile([P, 2 * HALVES, P], F32, name="ch%d" % b)
-            for s in range(2 * HALVES):
-                c = 2 * HALVES * b + s
-                nc.vector.tensor_scalar(ch[:, s, :], vis[:, s, :], tri_col[:, c : c + 1], None, ALU.mult)
-            lit = sb.tile([P, 2 * HALVES, P], F32, name="lit%d" % b)
-            nc.vector.scalar_tensor_tensor(lit[:], er_t[b][:], 0.1, ch[:], ALU.add, ALU.mult)
+                nc.tensor.matmul(z_t[d][:, h, :], y[:, d, h * P : (h + 1) * P], ident[:],
+                                 start=False, stop=(h == HALVES - 1), is_transpose=True)
+        for d in range(D):
+            vis = sb.tile([P, HALVES, P], F32, name="vis%d" % d, tag="vis%d" % d)
+            nc.scalar.activation(vis[:], z_t[d][:], ACT.Sigmoid, scale=-2.0)
+            ch = sb.tile([P, HALVES, P], F32, name="ch%d" % d)
+            for h in range(HALVES):
+                c = HALVES * d + h
+                nc.vector.tensor_scalar(ch[:, h, :], vis[:, h, :], tri_col[:, c : c + 1], None, ALU.mult)
+            lit = sb.tile([P, HALVES, P], F32, name="lit%d" % d)
+            s0 = (d % 2) * HALVES
+            nc.vector.scalar_tensor_tensor(lit[:], er_t[d // 2][:, s0 : s0 + HALVES, :], 0.1, ch[:], ALU.add, ALU.mult)
             for bank, terms in ((den, ch), (num, lit)):
-                for s in range(2 * HALVES):
-                    h = s % HALVES
-                    nc.tensor.matmul(bank[:, h * P : (h + 1) * P], terms[:, s, :], ident[:],
-                                     start=(b == 0 and s == 0), stop=(b == 1 and s == 2 * HALVES - 1),
+                for h in range(HALVES):
+                    nc.tensor.matmul(bank[:, h * P : (h + 1) * P], terms[:, h, :], ident[:],
+                                     start=(d == 0 and h == 0), stop=(d == D - 1 and h == HALVES - 1),
                                      is_transpose=True)
 
         log_den = sb.tile([P, V], F32, name="log_den")
         nc.scalar.activation(log_den[:], den[:], ACT.Ln, bias=0.02)
-        log_num = sb.tile([P, V], F32, name="log_num")
-        nc.scalar.activation(log_num[:], num[:], ACT.Ln, bias=0.002)
-        res = sb.tile([P, V], F32, name="res")
-        nc.vector.tensor_tensor(res[:], log_num[:], log_den[:], ALU.subtract)
-        nc.sync.dma_start(out, res[:])
+        for h in range(HALVES):
+            cols = slice(h * P, (h + 1) * P)
+            log_num = sb.tile([P, P], F32, name="log_num%d" % h)
+            nc.scalar.activation(log_num[:], num[:, cols], ACT.Ln, bias=0.002)
+            res = sb.tile([P, P], F32, name="res%d" % h)
+            nc.vector.tensor_tensor(res[:], log_num[:], log_den[:, cols], ALU.subtract)
+            nc.sync.dma_start(out[:, cols], res[:])

@@ -40,19 +40,20 @@ def tile_picked_yddgi_log_p_kernel(
         def load_words(g):
             nc.sync.dma_start(words[g][:].bitcast(I32), x_words[g].rearrange("p n t -> p (n t)").bitcast(I32))
 
+        load_words(0)
         for q in range(4):
             nc.sync.dma_start(
                 scales[32 * q : 32 * q + 4 * PASSES, :].bitcast(I32),
                 x_scales[:, 4 * q : 4 * q + 4, :].bitcast(I32),
             )
-        load_words(0)
-        load_words(1)
         raw = {}
         for i, w in enumerate((w1, w2)):
             tile = sb.tile([P, PASSES, PACK, M], F32, name="raw%d" % i)
             nc.sync.dma_start(tile[:], w.rearrange("(g p j) m -> p g j m", p=P, j=PACK))
             for g in range(PASSES):
                 raw[i, g] = tile[:, g]
+            if i == 0:
+                load_words(1)
         for g in range(PASSES):
             tile = sb.tile([P, PACK, M], F32, name="raw2_%d" % g)
             nc.sync.dma_start(tile[:], w3[g * 512 : (g + 1) * 512, :].rearrange("(p j) m -> p j m", j=PACK))
@@ -72,6 +73,8 @@ def tile_picked_yddgi_log_p_kernel(
         make_identity(nc, ident[:])
         neg_half = sb.tile([P, V], F32, name="neg_half")
         nc.gpsimd.memset(neg_half[:], -0.5)
+        tenth = sb.tile([P, V], F32, name="tenth")
+        nc.gpsimd.tensor_scalar(tenth[:], neg_half[:], -0.2, 0.0, ALU.mult, ALU.add)
         zero_exp = sb.tile([P, 1], F32, name="zero_exp", tag="mu")
         nc.gpsimd.memset(zero_exp[:], 0.0)
         one = sb.tile([P, 1], F32, name="one")
@@ -80,29 +83,35 @@ def tile_picked_yddgi_log_p_kernel(
         nc.gpsimd.memset(tiny[:], TINY)
 
         xs = sb.tile([P, S], U8, name="xs", align_bytes=64)
-        nc.vector.tensor_copy(xs[:], scales[:].indirect(offs_sb[:]))
         xw = []
-        for g in range(PASSES):
-            tile = sb.tile([P, S], U32, name="xw%d" % g, align_bytes=64)
+
+        def pick_words(g, tag):
+            tile = sb.tile([P, S], U32, name="xw%d" % g, tag=tag, align_bytes=64)
             nc.vector.tensor_copy(tile[:], words[g][:].indirect(offs_sb[:]))
             xw.append(tile)
 
-        acc = []
+        def quantise(i, g, tag):
+            grouped = sb.tile([P, M * PACK], BF16, name="grouped%d_%d" % (i, g), tag=tag, align_bytes=64)
+            dst = grouped[:].rearrange("p (c i t) -> p c t i", i=4, t=PACK)
+            src = raw[i, g].rearrange("p t (c i) -> p c t i", i=4)
+            if (i, g) == (2, PASSES - 1):
+                nc.vector.tensor_copy(dst, src)
+            else:
+                nc.scalar.copy(dst, src)
+            codes = sb.tile([P, M], U32, name="codes%d_%d" % (i, g), align_bytes=64)
+            wsc = sb.tile([P, M], U8, name="wsc%d_%d" % (i, g), align_bytes=64)
+            nc.vector.quantize_mx(out=codes[:].bitcast(FP8X4), scales=wsc[:], in_=grouped[:])
+            return codes, wsc
+
+        acc = [psum.tile([P, S], F32, name="acc%d" % i, tag="bank%d" % i) for i in range(3)]
+        tags = {(0, 0): "first", (1, 0): "last", (2, 1): "last"}
+        pick_words(0, "xw0")
+        nc.vector.tensor_copy(xs[:], scales[:].indirect(offs_sb[:]))
         for i in range(3):
-            bank = psum.tile([P, S], F32, name="acc%d" % i, tag="bank%d" % i)
             for g in range(PASSES):
-                grouped = sb.tile([P, M * PACK], BF16, name="grouped%d_%d" % (i, g), tag="grouped%d" % ((2 * i + g) % 3), align_bytes=64)
-                dst = grouped[:].rearrange("p (c i t) -> p c t i", i=4, t=PACK)
-                src = raw[i, g].rearrange("p t (c i) -> p c t i", i=4)
-                if g == 0:
-                    nc.scalar.copy(dst, src)
-                else:
-                    nc.vector.tensor_copy(dst, src)
-                codes = sb.tile([P, M], U32, name="codes%d_%d" % (i, g), align_bytes=64)
-                wsc = sb.tile([P, M], U8, name="wsc%d_%d" % (i, g), align_bytes=64)
-                nc.vector.quantize_mx(out=codes[:].bitcast(FP8X4), scales=wsc[:], in_=grouped[:])
+                codes, wsc = quantise(i, g, tags.get((i, g), "grouped%d_%d" % (i, g)))
                 nc.tensor.matmul_mx(
-                    out=bank[:],
+                    out=acc[i][:],
                     lhsT=codes[:].bitcast(FP8X4),
                     lhsT_scale=wsc[:],
                     rhs=xw[g][:].bitcast(FP8X4),
@@ -110,7 +119,8 @@ def tile_picked_yddgi_log_p_kernel(
                     start=(g == 0),
                     stop=(g == PASSES - 1),
                 )
-            acc.append(bank)
+                if (i, g) == (0, 0):
+                    pick_words(1, "first")
 
         er = sb.tile([P, S], F32, name="er")
         nc.scalar.activation(er[:], acc[0][:], ACT.Exp, bias=zero_exp[:], scale=0.5)
@@ -127,7 +137,7 @@ def tile_picked_yddgi_log_p_kernel(
         er_g = sb.tile([P, D, V], F32, name="er_g")
         er_t = [psum.tile([P, 2 * HALVES, P], F32, name="er_t%d" % b, tag="bank%d" % (3 + b)) for b in range(2)]
         for d in range(D):
-            nc.vector.tensor_copy(er_g[:, d, :], er[:].indirect(pos_sb[d][:]))
+            nc.vector.tensor_tensor(er_g[:, d, :], er[:].indirect(pos_sb[d][:]), tenth[:], ALU.add)
             for h in range(HALVES):
                 nc.tensor.transpose(er_t[d // 2][:, (d % 2) * HALVES + h, :], er_g[:, d, h * P : (h + 1) * P], ident[:])
 
@@ -175,25 +185,31 @@ def tile_picked_yddgi_log_p_kernel(
         for d in range(D):
             vis = sb.tile([P, HALVES, P], F32, name="vis%d" % d, tag="vis%d" % d)
             nc.scalar.activation(vis[:], z_t[d][:], ACT.Sigmoid, scale=-2.0)
-            ch = sb.tile([P, HALVES, P], F32, name="ch%d" % d)
-            for h in range(HALVES):
-                c = HALVES * d + h
-                nc.vector.tensor_scalar(ch[:, h, :], vis[:, h, :], tri_col[:, c : c + 1], None, ALU.mult)
+            pair = sb.tile([P, HALVES, P], F32, name="pair%d" % d)
             lit = sb.tile([P, HALVES, P], F32, name="lit%d" % d)
-            s0 = (d % 2) * HALVES
-            nc.vector.scalar_tensor_tensor(lit[:], er_t[d // 2][:, s0 : s0 + HALVES, :], 0.1, ch[:], ALU.add, ALU.mult)
-            for bank, terms in ((den, ch), (num, lit)):
-                for h in range(HALVES):
-                    nc.tensor.matmul(bank[:, h * P : (h + 1) * P], terms[:, h, :], ident[:],
-                                     start=(d == 0 and h == 0), stop=(d == D - 1 and h == HALVES - 1),
-                                     is_transpose=True)
+            for h in range(HALVES):
+                col = tri_col[:, HALVES * d + h : HALVES * d + h + 1]
+                nc.vector.scalar_tensor_tensor(
+                    lit[:, h, :], vis[:, h, :], col, er_t[d // 2][:, (d % 2) * HALVES + h, :], ALU.mult, ALU.mult
+                )
+                nc.tensor.matmul(num[:, h * P : (h + 1) * P], lit[:, h, :], ident[:],
+                                 start=(d == 0 and h == 0), stop=(d == D - 1 and h == HALVES - 1), is_transpose=True)
+            for h in range(HALVES):
+                col = tri_col[:, HALVES * d + h : HALVES * d + h + 1]
+                if d % 2 == 0:
+                    nc.vector.tensor_scalar(pair[:, h, :], vis[:, h, :], col, None, ALU.mult)
+                else:
+                    nc.vector.scalar_tensor_tensor(pair[:, h, :], vis[:, h, :], col, first[:, h, :], ALU.mult, ALU.add)
+                    nc.tensor.matmul(den[:, h * P : (h + 1) * P], pair[:, h, :], ident[:],
+                                     start=(d == 1 and h == 0), stop=(d == D - 1 and h == HALVES - 1), is_transpose=True)
+            first = pair
 
-        log_den = sb.tile([P, V], F32, name="log_den")
-        nc.scalar.activation(log_den[:], den[:], ACT.Ln, bias=0.02)
+        log_num = sb.tile([P, V], F32, name="log_num")
+        nc.scalar.activation(log_num[:], num[:], ACT.Ln, bias=0.002)
         for h in range(HALVES):
             cols = slice(h * P, (h + 1) * P)
-            log_num = sb.tile([P, P], F32, name="log_num%d" % h)
-            nc.scalar.activation(log_num[:], num[:, cols], ACT.Ln, bias=0.002)
+            log_den = sb.tile([P, P], F32, name="log_den%d" % h)
+            nc.scalar.activation(log_den[:], den[:, cols], ACT.Ln, bias=0.02)
             res = sb.tile([P, P], F32, name="res%d" % h)
-            nc.vector.tensor_tensor(res[:], log_num[:], log_den[:, cols], ALU.subtract)
+            nc.vector.tensor_tensor(res[:], log_num[:, cols], log_den[:], ALU.subtract)
             nc.sync.dma_start(out[:, cols], res[:])

@@ -120,6 +120,17 @@ def tile_picked_yddgi_log_p_kernel(
                     stop=(g == PASSES - 1),
                 )
                 if (i, g) == (0, 0):
+                    warm = psum.tile([P, S], F32, name="warm", tag="bank5")
+                    for width in (S, P):
+                        nc.tensor.matmul_mx(
+                            out=warm[:, :width],
+                            lhsT=codes[:].bitcast(FP8X4),
+                            lhsT_scale=wsc[:],
+                            rhs=xw[g][:, :width].bitcast(FP8X4),
+                            rhs_scale=xs[:, :width],
+                            start=True,
+                            stop=True,
+                        )
                     pick_words(1, "first")
 
         er = sb.tile([P, S], F32, name="er")

from contextlib import ExitStack

import concourse.mybir as mybir
from concourse.masks import make_identity

K, T, S, M, D, V = 1024, 1024, 512, 128, 4, 256
FLOPS = 3 * 2 * K * S * M
P = 128
PACK = 4
PASSES = K // (P * PACK)
HALVES = V // P
TINY = 2.0**-50

F32 = mybir.dt.float32
BF16 = mybir.dt.bfloat16
I32 = mybir.dt.int32
U32 = mybir.dt.uint32
U16 = mybir.dt.uint16
U8 = mybir.dt.uint8
FP8X4 = mybir.dt.float8_e4m3fn_x4
ALU = mybir.AluOpType
ACT = mybir.ActivationFunctionType


def tile_picked_yddgi_log_p_kernel(
    tc, x_words, x_scales, w1, w2, w3, tri, dist, offs, pos1, pos2, pos3, pos4, out
):
    nc = tc.nc
    with ExitStack() as ctx:
        lists = ctx.enter_context(tc.tile_pool(name="lists", bufs=1))
        sb = ctx.enter_context(tc.tile_pool(name="sb", bufs=1))
        psum = ctx.enter_context(tc.psum_pool(name="psum", bufs=1))

        offs_sb = lists.tile([P, S // 16], U16, name="offs_sb")
        nc.sync.dma_start(offs_sb[:], offs)
        scales = sb.tile([P, T], U8, name="scales")
        nc.gpsimd.memset(scales[:].bitcast(I32), 0)
        words = [sb.tile([P, T], U32, name="words%d" % g) for g in range(PASSES)]

        def load_words(g):
            nc.sync.dma_start(words[g][:].bitcast(I32), x_words[g].rearrange("p n t -> p (n t)").bitcast(I32))

        load_words(0)
        for q in range(4):
            nc.sync.dma_start(
                scales[32 * q : 32 * q + 4 * PASSES, :].bitcast(I32),
                x_scales[:, 4 * q : 4 * q + 4, :].bitcast(I32),
            )
        raw = {}
        for i, w in enumerate((w1, w2)):
            tile = sb.tile([P, PASSES, PACK, M], F32, name="raw%d" % i)
            nc.sync.dma_start(tile[:], w.rearrange("(g p j) m -> p g j m", p=P, j=PACK))
            for g in range(PASSES):
                raw[i, g] = tile[:, g]
            if i == 0:
                load_words(1)
        for g in range(PASSES):
            tile = sb.tile([P, PACK, M], F32, name="raw2_%d" % g)
            nc.sync.dma_start(tile[:], w3[g * 512 : (g + 1) * 512, :].rearrange("(p j) m -> p j m", j=PACK))
            raw[2, g] = tile[:]
        pos_sb = []
        for d, pos in enumerate((pos1, pos2, pos3, pos4)):
            tile = lists.tile([P, V // 16], U16, name="pos_sb%d" % d)
            nc.sync.dma_start(tile[:], pos)
            pos_sb.append(tile)
        dist_sb = sb.tile([P, D, V], F32, name="dist_sb")
        nc.sync.dma_start(dist_sb[:], dist.rearrange("d p v -> p d v"))
        tri_rows = sb.tile([P, P], F32, name="tri_rows")
        nc.gpsimd.memset(tri_rows[:], 0.0)
        nc.sync.dma_start(tri_rows[: D * HALVES, :], tri[:, 0, :].rearrange("d (h c) -> d h c", c=P))

        ident = sb.tile([P, P], F32, name="ident")
        make_identity(nc, ident[:])
        neg_half = sb.tile([P, V], F32, name="neg_half")
        nc.gpsimd.memset(neg_half[:], -0.5)
        tenth = sb.tile([P, V], F32, name="tenth")
        nc.gpsimd.tensor_scalar(tenth[:], neg_half[:], -0.2, 0.0, ALU.mult, ALU.add)
        zero_exp = sb.tile([P, 1], F32, name="zero_exp", tag="mu")
        nc.gpsimd.memset(zero_exp[:], 0.0)
        one = sb.tile([P, 1], F32, name="one")
        nc.scalar.activation(one[:], zero_exp[:], ACT.Exp, bias=zero_exp[:])
        tiny = sb.tile([P, 1], F32, name="tiny", tag="vis0")
        nc.gpsimd.memset(tiny[:], TINY)

        xs = sb.tile([P, S], U8, name="xs", align_bytes=64)
        xw = []

        def pick_words(g, tag):
            tile = sb.tile([P, S], U32, name="xw%d" % g, tag=tag, align_bytes=64)
            nc.vector.tensor_copy(tile[:], words[g][:].indirect(offs_sb[:]))
            xw.append(tile)

        def quantise(i, g, tag):
            grouped = sb.tile([P, M * PACK], BF16, name="grouped%d_%d" % (i, g), tag=tag, align_bytes=64)
            dst = grouped[:].rearrange("p (c i t) -> p c t i", i=4, t=PACK)
            src = raw[i, g].rearrange("p t (c i) -> p c t i", i=4)
            if (i, g) == (2, PASSES - 1):
                nc.vector.tensor_copy(dst, src)
            else:
                nc.scalar.copy(dst, src)
            codes = sb.tile([P, M], U32, name="codes%d_%d" % (i, g), align_bytes=64)
            wsc = sb.tile([P, M], U8, name="wsc%d_%d" % (i, g), align_bytes=64)
            nc.vector.quantize_mx(out=codes[:].bitcast(FP8X4), scales=wsc[:], in_=grouped[:])
            return codes, wsc

        acc = [psum.tile([P, S], F32, name="acc%d" % i, tag="bank%d" % i) for i in range(3)]
        tags = {(0, 0): "first", (1, 0): "last", (2, 1): "last"}
        pick_words(0, "xw0")
        nc.vector.tensor_copy(xs[:], scales[:].indirect(offs_sb[:]))
        for i in range(3):
            for g in range(PASSES):
                codes, wsc = quantise(i, g, tags.get((i, g), "grouped%d_%d" % (i, g)))
                nc.tensor.matmul_mx(
                    out=acc[i][:],
                    lhsT=codes[:].bitcast(FP8X4),
                    lhsT_scale=wsc[:],
                    rhs=xw[g][:].bitcast(FP8X4),
                    rhs_scale=xs[4 * g :, :],
                    start=(g == 0),
                    stop=(g == PASSES - 1),
                )
                if (i, g) == (0, 0):
                    warm = psum.tile([P, S], F32, name="warm", tag="bank5")
                    for width in (S, P):
                        nc.tensor.matmul_mx(
                            out=warm[:, :width],
                            lhsT=codes[:].bitcast(FP8X4),
                            lhsT_scale=wsc[:],
                            rhs=xw[g][:, :width].bitcast(FP8X4),
                            rhs_scale=xs[:, :width],
                            start=True,
                            stop=True,
                        )
                    pick_words(1, "first")

        er = sb.tile([P, S], F32, name="er")
        nc.scalar.activation(er[:], acc[0][:], ACT.Exp, bias=zero_exp[:], scale=0.5)
        e_mean = sb.tile([P, S], F32, name="e_mean")
        nc.scalar.activation(e_mean[:], acc[1][:], ACT.Exp, bias=zero_exp[:])
        e_msq = sb.tile([P, S], F32, name="e_msq")
        nc.scalar.activation(e_msq[:], acc[2][:], ACT.Exp, bias=zero_exp[:])

        tri_ps = psum.tile([P, P], F32, name="tri_ps", tag="bank2")
        nc.tensor.transpose(tri_ps[:], tri_rows[:], ident[:])
        tri_col = sb.tile([P, D * HALVES], F32, name="tri_col")
        nc.vector.tensor_copy(tri_col[:], tri_ps[:, : D * HALVES])

        er_g = sb.tile([P, D, V], F32, name="er_g")
        er_t = [psum.tile([P, 2 * HALVES, P], F32, name="er_t%d" % b, tag="bank%d" % (3 + b)) for b in range(2)]
        for d in range(D):
            nc.vector.tensor_tensor(er_g[:, d, :], er[:].indirect(pos_sb[d][:]), tenth[:], ALU.add)
            for h in range(HALVES):
                nc.tensor.transpose(er_t[d // 2][:, (d % 2) * HALVES + h, :], er_g[:, d, h * P : (h + 1) * P], ident[:])

        mu = sb.tile([P, S], F32, name="mu", tag="mu")
        nc.scalar.activation(mu[:], e_mean[:], ACT.Ln, bias=one[:])
        sp = sb.tile([P, S], F32, name="sp")
        nc.scalar.activation(sp[:], e_msq[:], ACT.Ln, bias=one[:])
        musq = sb.tile([P, S], F32, name="musq", tag="late_gap")
        nc.scalar.activation(musq[:], mu[:], ACT.Square)

        log_a = sb.tile([P, D, V], F32, name="log_a")

        def log_shadow(d, gap):
            nc.vector.tensor_tensor(gap, mu[:].indirect(pos_sb[d][:]), dist_sb[:, d, :], ALU.subtract)
            a = sb.tile([P, V], F32, name="a%d" % d)
            nc.vector.tensor_scalar(a[:], gap, -1.0, 0.0, ALU.mult, ALU.max)
            nc.scalar.activation(log_a[:, d, :], a[:], ACT.Ln, bias=tiny[:])

        early_gap = sb.tile([P, 2, V], F32, name="early_gap")
        for d in range(2):
            log_shadow(d, early_gap[:, d, :])
        diff = sb.tile([P, S], F32, name="diff")
        nc.vector.tensor_tensor(diff[:], musq[:], sp[:], ALU.subtract)
        adiff = sb.tile([P, S], F32, name="adiff")
        nc.scalar.activation(adiff[:], diff[:], ACT.Abs)
        log_var = sb.tile([P, S], F32, name="log_var")
        nc.scalar.activation(log_var[:], adiff[:], ACT.Ln, bias=0.05)
        late_gap = sb.tile([P, 2, V], F32, name="late_gap", tag="late_gap")
        for d in range(2, D):
            log_shadow(d, late_gap[:, d - 2, :])

        y = sb.tile([P, D, V], F32, name="y")
        num = psum.tile([P, V], F32, name="num", tag="bank5")
        den = psum.tile([P, V], F32, name="den", tag="bank6")
        z_t = [psum.tile([P, HALVES, P], F32, name="z_t%d" % d, tag="bank%d" % (0, 1, 2, 7)[d]) for d in range(D)]
        for d in range(D):
            for h in range(HALVES):
                nc.tensor.matmul(z_t[d][:, h, :], log_a[:, d, h * P : (h + 1) * P], ident[:],
                                 start=(h == 0), stop=False, is_transpose=True)
        for d in range(D):
            nc.vector.tensor_tensor(y[:, d, :], log_var[:].indirect(pos_sb[d][:]), neg_half[:], ALU.mult)
            for h in range(HALVES):
                nc.tensor.matmul(z_t[d][:, h, :], y[:, d, h * P : (h + 1) * P], ident[:],
                                 start=False, stop=(h == HALVES - 1), is_transpose=True)
        for d in range(D):
            vis = sb.tile([P, HALVES, P], F32, name="vis%d" % d, tag="vis%d" % d)
            nc.scalar.activation(vis[:], z_t[d][:], ACT.Sigmoid, scale=-2.0)
            pair = sb.tile([P, HALVES, P], F32, name="pair%d" % d)
            lit = sb.tile([P, HALVES, P], F32, name="lit%d" % d)
            for h in range(HALVES):
                col = tri_col[:, HALVES * d + h : HALVES * d + h + 1]
                nc.vector.scalar_tensor_tensor(
                    lit[:, h, :], vis[:, h, :], col, er_t[d // 2][:, (d % 2) * HALVES + h, :], ALU.mult, ALU.mult
                )
                nc.tensor.matmul(num[:, h * P : (h + 1) * P], lit[:, h, :], ident[:],
                                 start=(d == 0 and h == 0), stop=(d == D - 1 and h == HALVES - 1), is_transpose=True)
            for h in range(HALVES):
                col = tri_col[:, HALVES * d + h : HALVES * d + h + 1]
                if d % 2 == 0:
                    nc.vector.tensor_scalar(pair[:, h, :], vis[:, h, :], col, None, ALU.mult)
                else:
                    nc.vector.scalar_tensor_tensor(pair[:, h, :], vis[:, h, :], col, first[:, h, :], ALU.mult, ALU.add)
                    nc.tensor.matmul(den[:, h * P : (h + 1) * P], pair[:, h, :], ident[:],
                                     start=(d == 1 and h == 0), stop=(d == D - 1 and h == HALVES - 1), is_transpose=True)
            first = pair

        log_num = sb.tile([P, V], F32, name="log_num")
        nc.scalar.activation(log_num[:], num[:], ACT.Ln, bias=0.002)
        for h in range(HALVES):
            cols = slice(h * P, (h + 1) * P)
            log_den = sb.tile([P, P], F32, name="log_den%d" % h)
            nc.scalar.activation(log_den[:], den[:, cols], ACT.Ln, bias=0.02)
            res = sb.tile([P, P], F32, name="res%d" % h)
            nc.vector.tensor_tensor(res[:], log_num[:, cols], log_den[:], ALU.subtract)
            nc.sync.dma_start(out[:, cols], res[:])
